import numpy as np
import ml_dtypes


def mxq(x, axis, fmt="e4m3"):
    dtype, down = {"e4m3": (ml_dtypes.float8_e4m3fn, 7), "e5m2": (ml_dtypes.float8_e5m2, 14)}[fmt]
    v = np.moveaxis(np.asarray(x, np.float32).astype(ml_dtypes.bfloat16).astype(np.float64), axis, -1)
    blocks = v.reshape(v.shape[:-1] + (-1, 32))
    amax = np.abs(blocks).max(-1, keepdims=True)
    byte = np.maximum(np.where(amax > 0, np.frexp(amax)[1] - 1 + 127, 0) - down, 1)
    scale = np.exp2(byte - 127.0)
    codes = (blocks / scale).astype(np.float32).astype(dtype).astype(np.float64)
    return np.moveaxis((codes * scale).reshape(v.shape), -1, axis)


WIDE = False


def mx_kscale(k):
    if not WIDE:
        return np.ones(k)
    levels = np.array([10, -10, 5, -5, 0])
    if k % 512:
        return np.exp2(np.random.permutation(np.resize(levels, k // 32))).repeat(32)
    a = np.empty((k // 512, 16))
    for p in range(k // 512):
        a[p, :8] = np.random.permutation(np.resize(levels, 8))
        for g in range(8):
            far = levels[np.abs(levels - a[p, g]) >= 10]
            a[p, g + 8] = far[np.random.randint(len(far))]
    return np.exp2(a.ravel()).repeat(32)


def f64(x):
    return np.asarray(x).astype(np.float64)


def striped(idx):
    return np.tile(idx.reshape(-1, 16).T, (8, 1)).astype(np.uint16)


def unstriped(offs):
    return offs[:16].T.reshape(-1).astype(np.int64)


E2M1 = np.array([0.0, 0.5, 1.0, 1.5, 2.0, 3.0, 4.0, 6.0, -0.0, -0.5, -1.0, -1.5, -2.0, -3.0, -4.0, -6.0])


def pack_weight(w, fmt):
    k, n = w.shape
    w = f64(np.asarray(w, np.float32).astype(ml_dtypes.bfloat16)).reshape(k // 32, 32, n)
    amax = np.abs(w).max(1)
    if fmt == "e4m3":
        byte = np.frexp(amax)[1] - 1 + 127 - 7
    else:
        mant, ex = np.frexp(amax / 6.0)
        byte = np.where(mant > 0.5, ex, ex - 1) + 127
    byte = np.clip(np.where(amax > 0, byte, 1), 1, 254)
    scaled = (w * np.exp2(127.0 - byte)[:, None, :]).reshape(k, n).astype(np.float32)
    by_word = np.ascontiguousarray(scaled.reshape(k // 512, 128, 4, n).transpose(0, 1, 3, 2))
    if fmt == "e4m3":
        words = by_word.astype(ml_dtypes.float8_e4m3fn).view(np.uint8)
    else:
        c = by_word.astype(ml_dtypes.float4_e2m1fn).view(np.uint8) & 0xF
        words = (c[..., 0::2] | (c[..., 1::2] << 4)).reshape(k // 512, 128, 2 * n)
    return np.ascontiguousarray(words), np.ascontiguousarray(byte.astype(np.uint8).reshape(k // 512, 16, n))


def unpack_weight(words, scales, fmt):
    g, _, n = scales.shape
    words = np.ascontiguousarray(words).reshape(g, 128, n, -1)
    if fmt == "e4m3":
        vals = words.view(ml_dtypes.float8_e4m3fn).astype(np.float64)
    else:
        nib = np.empty((g, 128, n, 4), np.uint8)
        nib[..., 0::2] = words & 0xF
        nib[..., 1::2] = words >> 4
        vals = E2M1[nib]
    vals = vals * np.repeat(np.exp2(scales.astype(np.float64) - 127.0), 8, axis=1)[..., None]
    return vals.transpose(0, 1, 3, 2).reshape(g * 512, n)


def gelu(v):
    return 0.5 * v * (1.0 + np.tanh(np.sqrt(2.0 / np.pi) * (v + 0.044715 * v**3)))


def often(T, S):
    return np.random.permutation(T)[(T * np.random.uniform(0, 1, S) ** 4).astype(np.int64)]


K, K2, H, T, S, P = 512, 1024, 1024, 4096, 1024, 512

def setup_inputs():
    n = np.random.standard_normal
    s, s2, u = mx_kscale(K)[:, None], mx_kscale(K2)[:, None], mx_kscale(H)[:, None]
    d = {}
    d["tab_words"], d["tab_scales"] = pack_weight(n((K, T)) * s, "e4m3")
    d["tab2_words"], d["tab2_scales"] = pack_weight(n((K2, T)) * s2, "e4m3")
    d["tab3_words"], d["tab3_scales"] = pack_weight(n((K, T)) * s, "e4m3")
    d["offs"] = striped(np.random.permutation(T)[:S])
    d["offs2"] = striped(np.random.permutation(T)[:S])
    d["offs3"] = striped(np.random.permutation(T)[:S])
    d["pos1"] = striped(np.random.permutation(S)[:P])
    d["pos2"] = striped(often(S, P))
    d["pos3"] = striped(often(S, P))
    d["wa"] = (n((K, H)) / K ** 0.5 / s * u.T).astype(np.float32)
    d["wb_words"], d["wb_scales"] = pack_weight(1.1 * n((K2, H)) / K2 ** 0.5 / s2, "e2m1")
    d["wd_words"], d["wd_scales"] = pack_weight(n((K, H)) / K ** 0.5 / s * u.T, "e4m3")
    d["swing"] = np.random.uniform(2.0, 2.9, H).astype(np.float32)
    d["wz"] = (n((H, H)) / H ** 0.5 / u).astype(np.float32)
    d["keep"] = (np.random.uniform(0.5, 1.5, H) / u[:, 0]).astype(np.float32)
    return d

def reference(tab_words, tab_scales, tab2_words, tab2_scales, tab3_words, tab3_scales, offs, offs2, offs3, pos1, pos2, pos3, wa, wb_words, wb_scales, wd_words, wd_scales, swing, wz, keep):
    v = unpack_weight(tab_words, tab_scales, "e4m3")[:, unstriped(offs)]
    v2 = unpack_weight(tab2_words, tab2_scales, "e4m3")[:, unstriped(offs2)]
    v3 = unpack_weight(tab3_words, tab3_scales, "e4m3")[:, unstriped(offs3)]
    wb = unpack_weight(wb_words, wb_scales, "e2m1")
    wd = unpack_weight(wd_words, wd_scales, "e4m3")
    a = mxq(f64(wa), 0, "e4m3").T @ v
    b = f64(swing)[:, None] * np.tanh(wb.T @ v2)
    d = wd.T @ v3
    a1 = a[:, unstriped(pos1)]
    z = (a1 + d[:, unstriped(pos3)]) * np.cos(b[:, unstriped(pos2)])
    y = mxq(f64(wz), 0, "e4m3").T @ mxq(z, 0, "e4m3")
    return np.maximum(y, f64(keep)[:, None] * a1)

@@ -1,0 +1,280 @@
+import math
+from contextlib import ExitStack
+
+import concourse.mybir as mybir
+
+F32 = mybir.dt.float32
+BF16 = mybir.dt.bfloat16
+I32 = mybir.dt.int32
+U32 = mybir.dt.uint32
+U16 = mybir.dt.uint16
+U8 = mybir.dt.uint8
+E4M3 = mybir.dt.float8_e4m3fn_x4
+E2M1 = mybir.dt.float4_e2m1fn_x4
+ALU = mybir.AluOpType
+ACT = mybir.ActivationFunctionType
+
+P = 128
+T = 4096
+S = 1024
+H = 1024
+J = 512
+BANK = 512
+TILES = H // P
+HALF = J // 2
+
+FLOPS = 2 * (512 * H * S + 1024 * H * S + 512 * H * S + H * H * J)
+
+
+def tile_list_crane_lift_floor_kernel(
+    tc, tab_words, tab_scales, tab2_words, tab2_scales, tab3_words, tab3_scales,
+    offs, offs2, offs3, pos1, pos2, pos3,
+    wa, wb_words, wb_scales, wd_words, wd_scales, swing, wz, keep, out,
+):
+    nc = tc.nc
+    with ExitStack() as ctx:
+        lists = ctx.enter_context(tc.tile_pool(name="lists", bufs=1))
+        pool = ctx.enter_context(tc.tile_pool(name="pool", bufs=1))
+        psum = ctx.enter_context(tc.psum_pool(name="psum", bufs=8))
+
+        def held(name, shape, dtype):
+            return pool.tile(shape, dtype, name=name, tag=name, bufs=1, align_bytes=64)
+
+        def ring(tag, bufs, name, shape, dtype):
+            return pool.tile(shape, dtype, name=name, tag=tag, bufs=bufs, align_bytes=64)
+
+        def big(name, shape, dtype):
+            return ring("big", 4, name, shape, dtype)
+
+        def row4k(name, shape, dtype):
+            return ring("row4k", 10, name, shape, dtype)
+
+        def row2k(name, shape, dtype):
+            return ring("row2k", 8, name, shape, dtype)
+
+        def load_list(name, src):
+            t = lists.tile(list(src.shape), U16, name=name, tag=name)
+            nc.sync.dma_start(t[:], src)
+            return t
+
+        def words_i32(words, a):
+            return words[a].rearrange("p t i -> p (t i)").bitcast(I32)
+
+        warm_in = held("warm_in", [P, 1], F32)
+        warm_out = held("warm_out", [P, 1], F32)
+        nc.gpsimd.memset(warm_in[:], 0.0)
+        nc.scalar.activation(warm_out[:], warm_in[:], ACT.Silu)
+
+        sw1 = row4k("sw1", [P, T], U8)
+        sw2 = row4k("sw2", [P, T], U8)
+        sw3 = row4k("sw3", [P, T], U8)
+        nc.vector.memset(sw1[:].bitcast(I32), 0)
+        nc.vector.memset(sw3[:].bitcast(I32), 0)
+        nc.vector.memset(sw2[32:64, :].bitcast(I32), 0)
+        nc.vector.memset(sw2[64:128, :].bitcast(I32), 0)
+        planes = held("planes", [P, 6 * S], U8)
+        nc.vector.memset(planes[:].bitcast(I32), 0)
+        wsc_raw = held("wsc_raw", [P, 2 * H], U8)
+        nc.gpsimd.memset(wsc_raw[:].bitcast(I32), 0)
+
+        def load_weight(tile, rows, h):
+            nc.sync.dma_start(tile[:, h], rows[:, h * BANK:(h + 1) * BANK].rearrange("(p j) c -> p j c", j=4))
+
+        l_offs2 = load_list("l_offs2", offs2)
+        nc.sync.dma_start(sw2[0:32, :].bitcast(I32), tab2_scales.bitcast(I32).rearrange("a q n -> q a n"))
+        l_offs = load_list("l_offs", offs)
+        l_offs3 = load_list("l_offs3", offs3)
+        wa_raw = big("wa_raw", [P, 2, 4, BANK], F32)
+        load_weight(wa_raw, wa, 0)
+        nc.sync.dma_start(sw1[0:32:2, :].bitcast(I32), tab_scales[0].bitcast(I32))
+        nc.sync.dma_start(sw3[0:32:2, :].bitcast(I32), tab3_scales[0].bitcast(I32))
+        load_weight(wa_raw, wa, 1)
+        tw1 = big("tw1", [P, T], I32)
+        nc.sync.dma_start(tw1[:], words_i32(tab_words, 0))
+        wb_raw = row4k("wb_raw", [P, 2 * H], U16)
+        nc.sync.dma_start(wb_raw[:].bitcast(I32).rearrange("p (a n) -> p a n", a=2),
+                          wb_words.bitcast(I32).rearrange("a p n -> p a n"))
+        wd_raw = row4k("wd_raw", [P, H], I32)
+        nc.sync.dma_start(wd_raw[:], words_i32(wd_words, 0))
+        for q in range(4):
+            nc.gpsimd.dma_start(
+                wsc_raw[32 * q:32 * q + 4, :].bitcast(I32).rearrange("r (a n) -> r a n", a=2),
+                wb_scales[:, 4 * q:4 * q + 4, :].bitcast(I32).rearrange("a r n -> r a n"))
+            nc.gpsimd.dma_start(wsc_raw[32 * q + 4:32 * q + 8, 0:H].bitcast(I32),
+                                wd_scales[0, 4 * q:4 * q + 4, :].bitcast(I32))
+        l_pos1 = load_list("l_pos1", pos1)
+        l_pos2 = load_list("l_pos2", pos2)
+        l_pos3 = load_list("l_pos3", pos3)
+        swing_sb = held("swing_sb", [P, 2, 4], F32)
+        keep_sb = held("keep_sb", [P, 2, 4], F32)
+        nc.gpsimd.dma_start(swing_sb[:], swing.rearrange("(h p t) -> p h t", h=2, t=4))
+        nc.gpsimd.dma_start(keep_sb[:], keep.rearrange("(h p t) -> p h t", h=2, t=4))
+        tw2 = []
+        for a in range(2):
+            t = big("tw2_%d" % a, [P, T], I32)
+            nc.sync.dma_start(t[:], words_i32(tab2_words, a))
+            tw2.append(t)
+
+        gsc = held("gsc", [P, 3 * S], U8)
+        nc.vector.tensor_copy(gsc[:, 0:S], sw2[:].indirect(l_offs2[:]))
+        nc.vector.tensor_copy(gsc[:, S:2 * S], sw1[:].indirect(l_offs[:]))
+        nc.vector.tensor_copy(gsc[:, 2 * S:3 * S], sw3[:].indirect(l_offs3[:]))
+        for q in range(4):
+            nc.scalar.dma_start(
+                planes[32 * q:32 * q + 4, :].bitcast(I32).rearrange("r (a n) -> r a n", a=2),
+                gsc[8 * q:8 * q + 8, :].bitcast(I32))
+        sc2 = [planes[:, 0:S], planes[:, 3 * S:4 * S]]
+        sc1 = planes[:, S:2 * S]
+        sc3 = planes[:, 2 * S:3 * S]
+
+        wsc = held("wsc", [P, 2 * H], U8)
+        nc.vector.tensor_copy(wsc[:].rearrange("p (g t m) -> p g t m", g=4, t=4),
+                              wsc_raw[:].rearrange("p (g m t) -> p g t m", g=4, t=4))
+        wb_sb = held("wb_sb", [P, 2 * H], U16)
+        nc.vector.tensor_copy(wb_sb[:].rearrange("p (g t m) -> p g t m", g=4, t=4),
+                              wb_raw[:].rearrange("p (g m t) -> p g t m", g=4, t=4))
+        wd_sb = held("wd_sb", [P, H], I32)
+        nc.vector.tensor_copy(wd_sb[:].rearrange("p (g t c i) -> p g c t i", g=2, t=4, i=4),
+                              wd_raw[:].rearrange("p (g c i t) -> p g c t i", g=2, t=4, i=4))
+        turns = held("turns", [P, 2, 4], F32)
+        nc.vector.tensor_scalar(turns[:], swing_sb[:], 1.0 / (2.0 * math.pi), None, ALU.mult)
+
+        def round_weight(raw):
+            bf = ring("wbf", 2, "wbf", [P, 4 * BANK], BF16)
+            nc.scalar.copy(bf[:].rearrange("p (t m j) -> p m j t", t=4, j=4),
+                           raw.rearrange("p j (m t) -> p m j t", t=4))
+            return bf
+
+        def quantise(bf, codes, scales):
+            nc.vector.quantize_mx(out=codes.bitcast(E4M3), scales=scales, in_=bf)
+
+        def gather_words(name, table, idx):
+            g = held(name, [P, S], U32)
+            nc.vector.tensor_copy(g[:], table[:].bitcast(U32).indirect(idx[:]))
+            return g
+
+        def first_stage(i, passes, func, name):
+            cols = slice(i * P, (i + 1) * P)
+            win = row4k(name, [P, S], F32)
+            for half in range(S // BANK):
+                js = slice(half * BANK, (half + 1) * BANK)
+                acc = psum.tile([P, BANK], F32, name="acc", tag="acc")
+                for n, (w, ws, v, vs) in enumerate(passes):
+                    nc.tensor.matmul_mx(out=acc[:], lhsT=w(cols), lhsT_scale=ws(cols),
+                                        rhs=v[:, js].bitcast(E4M3), rhs_scale=vs[:, js],
+                                        start=(n == 0), stop=(n == len(passes) - 1))
+                nc.scalar.activation(win[:, js], acc[:], func)
+            return win
+
+        wa_q = held("wa_q", [P, H], U32)
+        wa_s = held("wa_s", [P, H], U8)
+        for h in range(2):
+            cs = slice(h * BANK, (h + 1) * BANK)
+            quantise(round_weight(wa_raw[:, h])[:], wa_q[:, cs], wa_s[:, cs])
+        v1 = gather_words("v1", tw1, l_offs)
+        tw3 = big("tw3", [P, T], I32)
+        nc.sync.dma_start(tw3[:], words_i32(tab3_words, 0))
+        a1 = []
+        v2 = []
+        for i in range(TILES):
+            win = first_stage(i, [(lambda c: wa_q[:, c].bitcast(E4M3), lambda c: wa_s[:, c], v1, sc1)],
+                              ACT.Copy, "win_a")
+            g = held("a1_%d" % i, [P, J], F32)
+            nc.vector.tensor_copy(g[:], win[:].indirect(l_pos1[:]))
+            a1.append(g)
+            if i in (1, 4):
+                a = len(v2)
+                v2.append(gather_words("v2_%d" % a, tw2[a], l_offs2))
+
+        wz_raw = []
+        for b in range(2):
+            t = big("wz_raw%d" % b, [P, 2, 4, BANK], F32)
+            for h in range(2):
+                load_weight(t, wz[b * 512:(b + 1) * 512, :], h)
+            wz_raw.append(t)
+
+        b_passes = [(lambda c, a=a: wb_sb[:, a * H + c.start:a * H + c.stop].bitcast(E2M1),
+                     lambda c, a=a: wsc[:, a * H + c.start:a * H + c.stop], v2[a], sc2[a]) for a in range(2)]
+        sq = [held("sq_%d" % b, [P, 4, J], F32) for b in range(2)]
+        picked = {}
+        whole = {}
+        v3 = None
+        for step in range(TILES + 2):
+            if step < TILES:
+                win = first_stage(step, b_passes, ACT.Tanh, "win_b")
+                picked[step] = row2k("picked", [P, J], F32)
+                nc.vector.tensor_copy(picked[step][:], win[:].indirect(l_pos2[:]))
+            i = step - 1
+            if 0 <= i < TILES:
+                whole[i] = row2k("whole", [P, J], I32)
+                nc.vector.tensor_scalar(whole[i][:], picked[i][:], turns[:, i // 4, i % 4:i % 4 + 1], None, ALU.mult)
+            i = step - 2
+            if 0 <= i < TILES:
+                frac = row2k("frac", [P, J], F32)
+                nc.vector.scalar_tensor_tensor(frac[:], picked[i][:], turns[:, i // 4, i % 4:i % 4 + 1],
+                                               whole[i][:], ALU.mult, ALU.subtract)
+                half_sin = row2k("half_sin", [P, J], F32)
+                nc.scalar.activation(half_sin[:], frac[:], ACT.Sin, scale=math.pi)
+                nc.scalar.activation(sq[i // 4][:, i % 4, :], half_sin[:], ACT.Square)
+            if step == 3:
+                v3 = gather_words("v3", tw3, l_offs3)
+
+        d_pass = [(lambda c: wd_sb[:, c].bitcast(E4M3), lambda c: wsc[4:P, c], v3, sc3)]
+        d_win = [first_stage(i, d_pass, ACT.Copy, "win_d") for i in range(TILES)]
+
+        wz_q = held("wz_q", [P, 2 * H], U32)
+        wz_s = held("wz_s", [P, 2 * H], U8)
+        for b in range(2):
+            for h in range(2):
+                cs = slice(b * H + h * BANK, b * H + (h + 1) * BANK)
+                quantise(round_weight(wz_raw[b][:, h])[:], wz_q[:, cs], wz_s[:, cs])
+
+        out_v = out.rearrange("(h m t) j -> h m t j", h=2, t=4)
+
+        def join(half):
+            js = slice(half * HALF, (half + 1) * HALF)
+            idx = l_pos3[:, half * (HALF // 16):(half + 1) * (HALF // 16)]
+            zq = []
+            for b in range(2):
+                z32 = ring("z32", 2, "z32", [P, 4, HALF], F32)
+                sums = ring("sum", 2, "sum", [P, 4, HALF], F32)
+                for t in range(4):
+                    i = 4 * b + t
+                    nc.vector.tensor_tensor(sums[:, t, :], d_win[i][:].indirect(idx), a1[i][:, js], ALU.add)
+                nc.vector.scalar_tensor_tensor(z32[:], sq[b][:, :, js], 0.5, sums[:], ALU.subtract, ALU.mult)
+                zbf = row2k("zbf", [P, 4 * HALF], BF16)
+                nc.scalar.activation(zbf[:].rearrange("p (c i t) -> p c t i", i=4, t=4),
+                                     z32[:].rearrange("p t (c i) -> p c t i", i=4), ACT.Copy, scale=-2.0)
+                codes = held("z_q%d%d" % (half, b), [P, HALF], U32)
+                scales = held("z_s%d%d" % (half, b), [P, HALF], U8)
+                zq.append((zbf, codes, scales))
+            return zq
+
+        def finish(half, zq):
+            js = slice(half * HALF, (half + 1) * HALF)
+            for pair in range(TILES // 2):
+                acc = psum.tile([P, BANK], F32, name="acc", tag="acc")
+                res = row2k("res", [P, 2, HALF], F32)
+                for u in range(2):
+                    i = 2 * pair + u
+                    for b in range(2):
+                        cs = slice(b * H + i * P, b * H + (i + 1) * P)
+                        nc.tensor.matmul_mx(out=acc[:, u * HALF:(u + 1) * HALF],
+                                            lhsT=wz_q[:, cs].bitcast(E4M3), lhsT_scale=wz_s[:, cs],
+                                            rhs=zq[b][1][:].bitcast(E4M3), rhs_scale=zq[b][2][:],
+                                            start=(b == 0), stop=(b == 1))
+                for u in range(2):
+                    i = 2 * pair + u
+                    nc.vector.scalar_tensor_tensor(res[:, u, :], a1[i][:, js], keep_sb[:, i // 4, i % 4:i % 4 + 1],
+                                                   acc[:, u * HALF:(u + 1) * HALF], ALU.mult, ALU.max)
+                t0 = 2 * (pair % 2)
+                nc.sync.dma_start(out_v[pair // 2, :, t0:t0 + 2, js], res[:])
+
+        z0 = join(0)
+        quantise(z0[0][0][:], z0[0][1][:], z0[0][2][:])
+        z1 = join(1)
+        quantise(z0[1][0][:], z0[1][1][:], z0[1][2][:])
+        quantise(z1[0][0][:], z1[0][1][:], z1[0][2][:])
+        finish(0, z0)
+        quantise(z1[1][0][:], z1[1][1][:], z1[1][2][:])
+        finish(1, z1)

@@ -69,13 +69,13 @@ def tile_list_crane_lift_floor_kernel(
         sw2 = row4k("sw2", [P, T], U8)
         sw3 = row4k("sw3", [P, T], U8)
         nc.vector.memset(sw1[:].bitcast(I32), 0)
-        nc.vector.memset(sw3[:].bitcast(I32), 0)
+        nc.gpsimd.memset(sw3[:].bitcast(I32), 0)
         nc.vector.memset(sw2[32:64, :].bitcast(I32), 0)
         nc.vector.memset(sw2[64:128, :].bitcast(I32), 0)
         planes = held("planes", [P, 6 * S], U8)
-        nc.vector.memset(planes[:].bitcast(I32), 0)
         wsc_raw = held("wsc_raw", [P, 2 * H], U8)
         nc.gpsimd.memset(wsc_raw[:].bitcast(I32), 0)
+        nc.gpsimd.memset(planes[:].bitcast(I32), 0)
 
         def load_weight(tile, rows, h):
             nc.sync.dma_start(tile[:, h], rows[:, h * BANK:(h + 1) * BANK].rearrange("(p j) c -> p j c", j=4))
@@ -97,18 +97,18 @@ def tile_list_crane_lift_floor_kernel(
         wd_raw = row4k("wd_raw", [P, H], I32)
         nc.sync.dma_start(wd_raw[:], words_i32(wd_words, 0))
         for q in range(4):
-            nc.gpsimd.dma_start(
+            nc.scalar.dma_start(
                 wsc_raw[32 * q:32 * q + 4, :].bitcast(I32).rearrange("r (a n) -> r a n", a=2),
                 wb_scales[:, 4 * q:4 * q + 4, :].bitcast(I32).rearrange("a r n -> r a n"))
-            nc.gpsimd.dma_start(wsc_raw[32 * q + 4:32 * q + 8, 0:H].bitcast(I32),
+            nc.scalar.dma_start(wsc_raw[32 * q + 4:32 * q + 8, 0:H].bitcast(I32),
                                 wd_scales[0, 4 * q:4 * q + 4, :].bitcast(I32))
         l_pos1 = load_list("l_pos1", pos1)
         l_pos2 = load_list("l_pos2", pos2)
         l_pos3 = load_list("l_pos3", pos3)
         swing_sb = held("swing_sb", [P, 2, 4], F32)
         keep_sb = held("keep_sb", [P, 2, 4], F32)
-        nc.gpsimd.dma_start(swing_sb[:], swing.rearrange("(h p t) -> p h t", h=2, t=4))
-        nc.gpsimd.dma_start(keep_sb[:], keep.rearrange("(h p t) -> p h t", h=2, t=4))
+        nc.sync.dma_start(swing_sb[:], swing.rearrange("(h p t) -> p h t", h=2, t=4))
+        nc.sync.dma_start(keep_sb[:], keep.rearrange("(h p t) -> p h t", h=2, t=4))
         tw2 = []
         for a in range(2):
             t = big("tw2_%d" % a, [P, T], I32)
@@ -195,32 +195,30 @@ def tile_list_crane_lift_floor_kernel(
 
         b_passes = [(lambda c, a=a: wb_sb[:, a * H + c.start:a * H + c.stop].bitcast(E2M1),
                      lambda c, a=a: wsc[:, a * H + c.start:a * H + c.stop], v2[a], sc2[a]) for a in range(2)]
+        b_win = [first_stage(i, b_passes, ACT.Tanh, "win_b") for i in range(TILES)]
+        v3 = gather_words("v3", tw3, l_offs3)
+        d_pass = [(lambda c: wd_sb[:, c].bitcast(E4M3), lambda c: wsc[4:P, c], v3, sc3)]
+        d_win = []
         sq = [held("sq_%d" % b, [P, 4, J], F32) for b in range(2)]
         picked = {}
         whole = {}
-        v3 = None
         for step in range(TILES + 2):
             if step < TILES:
-                win = first_stage(step, b_passes, ACT.Tanh, "win_b")
                 picked[step] = row2k("picked", [P, J], F32)
-                nc.vector.tensor_copy(picked[step][:], win[:].indirect(l_pos2[:]))
+                nc.vector.tensor_copy(picked[step][:], b_win[step][:].indirect(l_pos2[:]))
+                d_win.append(first_stage(step, d_pass, ACT.Copy, "win_d"))
             i = step - 1
             if 0 <= i < TILES:
                 whole[i] = row2k("whole", [P, J], I32)
                 nc.vector.tensor_scalar(whole[i][:], picked[i][:], turns[:, i // 4, i % 4:i % 4 + 1], None, ALU.mult)
             i = step - 2
             if 0 <= i < TILES:
-                frac = row2k("frac", [P, J], F32)
-                nc.vector.scalar_tensor_tensor(frac[:], picked[i][:], turns[:, i // 4, i % 4:i % 4 + 1],
+                nc.vector.scalar_tensor_tensor(sq[i // 4][:, i % 4, :], picked[i][:],
+                                               turns[:, i // 4, i % 4:i % 4 + 1],
                                                whole[i][:], ALU.mult, ALU.subtract)
-                half_sin = row2k("half_sin", [P, J], F32)
-                nc.scalar.activation(half_sin[:], frac[:], ACT.Sin, scale=math.pi)
-                nc.scalar.activation(sq[i // 4][:, i % 4, :], half_sin[:], ACT.Square)
-            if step == 3:
-                v3 = gather_words("v3", tw3, l_offs3)
-
-        d_pass = [(lambda c: wd_sb[:, c].bitcast(E4M3), lambda c: wsc[4:P, c], v3, sc3)]
-        d_win = [first_stage(i, d_pass, ACT.Copy, "win_d") for i in range(TILES)]
+        for b in range(2):
+            nc.scalar.activation(sq[b][:], sq[b][:], ACT.Abs)
+            nc.scalar.activation(sq[b][:], sq[b][:], ACT.Sin, scale=-2.0 * math.pi, bias=math.pi / 2.0)
 
         wz_q = held("wz_q", [P, 2 * H], U32)
         wz_s = held("wz_s", [P, 2 * H], U8)
@@ -241,10 +239,10 @@ def tile_list_crane_lift_floor_kernel(
                 for t in range(4):
                     i = 4 * b + t
                     nc.vector.tensor_tensor(sums[:, t, :], d_win[i][:].indirect(idx), a1[i][:, js], ALU.add)
-                nc.vector.scalar_tensor_tensor(z32[:], sq[b][:, :, js], 0.5, sums[:], ALU.subtract, ALU.mult)
+                nc.vector.tensor_tensor(z32[:], sq[b][:, :, js], sums[:], ALU.mult)
                 zbf = row2k("zbf", [P, 4 * HALF], BF16)
-                nc.scalar.activation(zbf[:].rearrange("p (c i t) -> p c t i", i=4, t=4),
-                                     z32[:].rearrange("p t (c i) -> p c t i", i=4), ACT.Copy, scale=-2.0)
+                nc.scalar.copy(zbf[:].rearrange("p (c i t) -> p c t i", i=4, t=4),
+                               z32[:].rearrange("p t (c i) -> p c t i", i=4))
                 codes = held("z_q%d%d" % (half, b), [P, HALF], U32)
                 scales = held("z_s%d%d" % (half, b), [P, HALF], U8)
                 zq.append((zbf, codes, scales))

@@ -174,14 +174,13 @@ def tile_list_crane_lift_floor_kernel(
         v1 = gather_words("v1", tw1, l_offs)
         tw3 = big("tw3", [P, T], I32)
         nc.sync.dma_start(tw3[:], words_i32(tab3_words, 0))
-        a1 = []
+        a1_group = [held("a1_%d" % b, [P, 4, J], F32) for b in range(2)]
+        a1 = [a1_group[i // 4][:, i % 4, :] for i in range(TILES)]
         v2 = []
         for i in range(TILES):
             win = first_stage(i, [(lambda c: wa_q[:, c].bitcast(E4M3), lambda c: wa_s[:, c], v1, sc1)],
                               ACT.Copy, "win_a")
-            g = held("a1_%d" % i, [P, J], F32)
-            nc.vector.tensor_copy(g[:], win[:].indirect(l_pos1[:]))
-            a1.append(g)
+            nc.vector.tensor_copy(a1[i], win[:].indirect(l_pos1[:]))
             if i in (1, 4):
                 a = len(v2)
                 v2.append(gather_words("v2_%d" % a, tw2[a], l_offs2))
@@ -200,6 +199,22 @@ def tile_list_crane_lift_floor_kernel(
         d_pass = [(lambda c: wd_sb[:, c].bitcast(E4M3), lambda c: wsc[4:P, c], v3, sc3)]
         d_win = []
         sq = [held("sq_%d" % b, [P, 4, J], F32) for b in range(2)]
+        wz_q = held("wz_q", [P, 2 * H], U32)
+        wz_s = held("wz_s", [P, 2 * H], U8)
+        wz_bf = {}
+
+        def round_wz(n):
+            wz_bf[n] = round_weight(wz_raw[n // 2][:, n % 2])
+
+        def quantise_wz(n):
+            cs = slice(n * BANK, (n + 1) * BANK)
+            quantise(wz_bf[n][:], wz_q[:, cs], wz_s[:, cs])
+
+        def cosine(half, b):
+            part = sq[b][:, :, half * HALF:(half + 1) * HALF]
+            nc.scalar.activation(part, part, ACT.Abs)
+            nc.scalar.activation(part, part, ACT.Sin, scale=-2.0 * math.pi, bias=math.pi / 2.0)
+
         picked = {}
         whole = {}
         for step in range(TILES + 2):
@@ -207,72 +222,89 @@ def tile_list_crane_lift_floor_kernel(
                 picked[step] = row2k("picked", [P, J], F32)
                 nc.vector.tensor_copy(picked[step][:], b_win[step][:].indirect(l_pos2[:]))
                 d_win.append(first_stage(step, d_pass, ACT.Copy, "win_d"))
+            if step in (2, 4, 7):
+                round_wz(len(wz_bf))
             i = step - 1
             if 0 <= i < TILES:
                 whole[i] = row2k("whole", [P, J], I32)
-                nc.vector.tensor_scalar(whole[i][:], picked[i][:], turns[:, i // 4, i % 4:i % 4 + 1], None, ALU.mult)
+                nc.gpsimd.tensor_scalar(whole[i][:], picked[i][:], turns[:, i // 4, i % 4:i % 4 + 1], 0.0,
+                                        ALU.mult, ALU.add)
             i = step - 2
             if 0 <= i < TILES:
                 nc.vector.scalar_tensor_tensor(sq[i // 4][:, i % 4, :], picked[i][:],
                                                turns[:, i // 4, i % 4:i % 4 + 1],
                                                whole[i][:], ALU.mult, ALU.subtract)
-        for b in range(2):
-            nc.scalar.activation(sq[b][:], sq[b][:], ACT.Abs)
-            nc.scalar.activation(sq[b][:], sq[b][:], ACT.Sin, scale=-2.0 * math.pi, bias=math.pi / 2.0)
-
-        wz_q = held("wz_q", [P, 2 * H], U32)
-        wz_s = held("wz_s", [P, 2 * H], U8)
-        for b in range(2):
-            for h in range(2):
-                cs = slice(b * H + h * BANK, b * H + (h + 1) * BANK)
-                quantise(round_weight(wz_raw[b][:, h])[:], wz_q[:, cs], wz_s[:, cs])
+            if step == 4:
+                quantise_wz(0)
+            if step == 6:
+                quantise_wz(1)
 
         out_v = out.rearrange("(h m t) j -> h m t j", h=2, t=4)
 
-        def join(half):
+        def join(half, b, sums):
             js = slice(half * HALF, (half + 1) * HALF)
             idx = l_pos3[:, half * (HALF // 16):(half + 1) * (HALF // 16)]
-            zq = []
-            for b in range(2):
-                z32 = ring("z32", 2, "z32", [P, 4, HALF], F32)
-                sums = ring("sum", 2, "sum", [P, 4, HALF], F32)
-                for t in range(4):
-                    i = 4 * b + t
-                    nc.vector.tensor_tensor(sums[:, t, :], d_win[i][:].indirect(idx), a1[i][:, js], ALU.add)
-                nc.vector.tensor_tensor(z32[:], sq[b][:, :, js], sums[:], ALU.mult)
-                zbf = row2k("zbf", [P, 4 * HALF], BF16)
-                nc.scalar.copy(zbf[:].rearrange("p (c i t) -> p c t i", i=4, t=4),
-                               z32[:].rearrange("p t (c i) -> p c t i", i=4))
-                codes = held("z_q%d%d" % (half, b), [P, HALF], U32)
-                scales = held("z_s%d%d" % (half, b), [P, HALF], U8)
-                zq.append((zbf, codes, scales))
-            return zq
+            z32 = ring("z32", 2, "z32", [P, 4, HALF], F32)
+            for t in range(4):
+                i = 4 * b + t
+                nc.vector.tensor_tensor(sums[:, t, :], d_win[i][:].indirect(idx), a1[i][:, js], ALU.add)
+            nc.vector.tensor_tensor(z32[:], sq[b][:, :, js], sums, ALU.mult)
+            zbf = row2k("zbf", [P, 4 * HALF], BF16)
+            nc.scalar.copy(zbf[:].rearrange("p (c i t) -> p c t i", i=4, t=4),
+                           z32[:].rearrange("p t (c i) -> p c t i", i=4))
+            codes = held("z_q%d%d" % (half, b), [P, HALF], U32)
+            scales = held("z_s%d%d" % (half, b), [P, HALF], U8)
+            return zbf, codes, scales
 
-        def finish(half, zq):
+        def fresh_sums():
+            return ring("sum", 2, "sum", [P, 4, HALF], F32)[:]
+
+        def product(acc, i, b, zq):
+            cs = slice(b * H + i * P, b * H + (i + 1) * P)
+            nc.tensor.matmul_mx(out=acc, lhsT=wz_q[:, cs].bitcast(E4M3), lhsT_scale=wz_s[:, cs],
+                                rhs=zq[b][1][:].bitcast(E4M3), rhs_scale=zq[b][2][:],
+                                start=(b == 0), stop=(b == 1))
+
+        def floor_and_store(half, accs, pairs):
             js = slice(half * HALF, (half + 1) * HALF)
-            for pair in range(TILES // 2):
-                acc = psum.tile([P, BANK], F32, name="acc", tag="acc")
+            for pair in pairs:
                 res = row2k("res", [P, 2, HALF], F32)
                 for u in range(2):
                     i = 2 * pair + u
-                    for b in range(2):
-                        cs = slice(b * H + i * P, b * H + (i + 1) * P)
-                        nc.tensor.matmul_mx(out=acc[:, u * HALF:(u + 1) * HALF],
-                                            lhsT=wz_q[:, cs].bitcast(E4M3), lhsT_scale=wz_s[:, cs],
-                                            rhs=zq[b][1][:].bitcast(E4M3), rhs_scale=zq[b][2][:],
-                                            start=(b == 0), stop=(b == 1))
-                for u in range(2):
-                    i = 2 * pair + u
                     nc.vector.scalar_tensor_tensor(res[:, u, :], a1[i][:, js], keep_sb[:, i // 4, i % 4:i % 4 + 1],
-                                                   acc[:, u * HALF:(u + 1) * HALF], ALU.mult, ALU.max)
+                                                   accs[i], ALU.mult, ALU.max)
                 t0 = 2 * (pair % 2)
                 nc.sync.dma_start(out_v[pair // 2, :, t0:t0 + 2, js], res[:])
 
-        z0 = join(0)
+        cosine(0, 0)
+        quantise_wz(2)
+        round_wz(3)
+        cosine(0, 1)
+        z0 = [join(0, 0, fresh_sums())]
+        quantise_wz(3)
+        cosine(1, 0)
+        z0.append(join(0, 1, fresh_sums()))
         quantise(z0[0][0][:], z0[0][1][:], z0[0][2][:])
-        z1 = join(1)
+        cosine(1, 1)
+        z1 = [join(1, 0, fresh_sums())]
         quantise(z0[1][0][:], z0[1][1][:], z0[1][2][:])
+        accs0 = []
+        for pair in range(TILES // 2):
+            bank = psum.tile([P, BANK], F32, name="acc", tag="acc")
+            for u in range(2):
+                accs0.append(bank[:, u * HALF:(u + 1) * HALF])
+                for b in range(2):
+                    product(accs0[-1], 2 * pair + u, b, z0)
+        floor_and_store(0, accs0, (0, 1))
         quantise(z1[0][0][:], z1[0][1][:], z1[0][2][:])
-        finish(0, z0)
+        z1.append(join(1, 1, a1_group[0][:, :, 0:HALF]))
+        floor_and_store(0, accs0, (2, 3))
+        accs1 = []
+        for i in range(TILES):
+            bank = psum.tile([P, BANK], F32, name="acc", tag="acc")
+            accs1.append(bank[:, 0:HALF])
+            product(accs1[i], i, 0, z1)
         quantise(z1[1][0][:], z1[1][1][:], z1[1][2][:])
-        finish(1, z1)
+        for i in range(TILES):
+            product(accs1[i], i, 1, z1)
+        floor_and_store(1, accs1, range(TILES // 2))

import math
from contextlib import ExitStack

import concourse.mybir as mybir

F32 = mybir.dt.float32
BF16 = mybir.dt.bfloat16
I32 = mybir.dt.int32
U32 = mybir.dt.uint32
U16 = mybir.dt.uint16
U8 = mybir.dt.uint8
E4M3 = mybir.dt.float8_e4m3fn_x4
E2M1 = mybir.dt.float4_e2m1fn_x4
ALU = mybir.AluOpType
ACT = mybir.ActivationFunctionType

P = 128
T = 4096
S = 1024
H = 1024
J = 512
BANK = 512
TILES = H // P
HALF = J // 2

FLOPS = 2 * (512 * H * S + 1024 * H * S + 512 * H * S + H * H * J)


def tile_list_crane_lift_floor_kernel(
    tc, tab_words, tab_scales, tab2_words, tab2_scales, tab3_words, tab3_scales,
    offs, offs2, offs3, pos1, pos2, pos3,
    wa, wb_words, wb_scales, wd_words, wd_scales, swing, wz, keep, out,
):
    nc = tc.nc
    with ExitStack() as ctx:
        lists = ctx.enter_context(tc.tile_pool(name="lists", bufs=1))
        pool = ctx.enter_context(tc.tile_pool(name="pool", bufs=1))
        psum = ctx.enter_context(tc.psum_pool(name="psum", bufs=8))

        def held(name, shape, dtype):
            return pool.tile(shape, dtype, name=name, tag=name, bufs=1, align_bytes=64)

        def ring(tag, bufs, name, shape, dtype):
            return pool.tile(shape, dtype, name=name, tag=tag, bufs=bufs, align_bytes=64)

        def big(name, shape, dtype):
            return ring("big", 4, name, shape, dtype)

        def row4k(name, shape, dtype):
            return ring("row4k", 10, name, shape, dtype)

        def row2k(name, shape, dtype):
            return ring("row2k", 8, name, shape, dtype)

        def load_list(name, src):
            t = lists.tile(list(src.shape), U16, name=name, tag=name)
            nc.sync.dma_start(t[:], src)
            return t

        def words_i32(words, a):
            return words[a].rearrange("p t i -> p (t i)").bitcast(I32)

        warm_in = held("warm_in", [P, 1], F32)
        warm_out = held("warm_out", [P, 1], F32)
        nc.gpsimd.memset(warm_in[:], 0.0)
        nc.scalar.activation(warm_out[:], warm_in[:], ACT.Silu)

        sw1 = row4k("sw1", [P, T], U8)
        sw2 = row4k("sw2", [P, T], U8)
        sw3 = row4k("sw3", [P, T], U8)
        nc.vector.memset(sw1[:].bitcast(I32), 0)
        nc.gpsimd.memset(sw3[:].bitcast(I32), 0)
        nc.vector.memset(sw2[32:64, :].bitcast(I32), 0)
        nc.vector.memset(sw2[64:128, :].bitcast(I32), 0)
        planes = held("planes", [P, 6 * S], U8)
        wsc_raw = held("wsc_raw", [P, 2 * H], U8)
        nc.gpsimd.memset(wsc_raw[:].bitcast(I32), 0)
        nc.gpsimd.memset(planes[:].bitcast(I32), 0)

        def load_weight(tile, rows, h):
            nc.sync.dma_start(tile[:, h], rows[:, h * BANK:(h + 1) * BANK].rearrange("(p j) c -> p j c", j=4))

        l_offs2 = load_list("l_offs2", offs2)
        nc.sync.dma_start(sw2[0:32, :].bitcast(I32), tab2_scales.bitcast(I32).rearrange("a q n -> q a n"))
        l_offs = load_list("l_offs", offs)
        l_offs3 = load_list("l_offs3", offs3)
        wa_raw = big("wa_raw", [P, 2, 4, BANK], F32)
        load_weight(wa_raw, wa, 0)
        nc.sync.dma_start(sw1[0:32:2, :].bitcast(I32), tab_scales[0].bitcast(I32))
        nc.sync.dma_start(sw3[0:32:2, :].bitcast(I32), tab3_scales[0].bitcast(I32))
        load_weight(wa_raw, wa, 1)
        tw1 = big("tw1", [P, T], I32)
        nc.sync.dma_start(tw1[:], words_i32(tab_words, 0))
        wb_raw = row4k("wb_raw", [P, 2 * H], U16)
        nc.sync.dma_start(wb_raw[:].bitcast(I32).rearrange("p (a n) -> p a n", a=2),
                          wb_words.bitcast(I32).rearrange("a p n -> p a n"))
        wd_raw = row4k("wd_raw", [P, H], I32)
        nc.sync.dma_start(wd_raw[:], words_i32(wd_words, 0))
        for q in range(4):
            nc.scalar.dma_start(
                wsc_raw[32 * q:32 * q + 4, :].bitcast(I32).rearrange("r (a n) -> r a n", a=2),
                wb_scales[:, 4 * q:4 * q + 4, :].bitcast(I32).rearrange("a r n -> r a n"))
            nc.scalar.dma_start(wsc_raw[32 * q + 4:32 * q + 8, 0:H].bitcast(I32),
                                wd_scales[0, 4 * q:4 * q + 4, :].bitcast(I32))
        l_pos1 = load_list("l_pos1", pos1)
        l_pos2 = load_list("l_pos2", pos2)
        l_pos3 = load_list("l_pos3", pos3)
        swing_sb = held("swing_sb", [P, 2, 4], F32)
        keep_sb = held("keep_sb", [P, 2, 4], F32)
        nc.sync.dma_start(swing_sb[:], swing.rearrange("(h p t) -> p h t", h=2, t=4))
        nc.sync.dma_start(keep_sb[:], keep.rearrange("(h p t) -> p h t", h=2, t=4))
        tw2 = []
        for a in range(2):
            t = big("tw2_%d" % a, [P, T], I32)
            nc.sync.dma_start(t[:], words_i32(tab2_words, a))
            tw2.append(t)

        gsc = held("gsc", [P, 3 * S], U8)
        nc.vector.tensor_copy(gsc[:, 0:S], sw2[:].indirect(l_offs2[:]))
        nc.vector.tensor_copy(gsc[:, S:2 * S], sw1[:].indirect(l_offs[:]))
        nc.vector.tensor_copy(gsc[:, 2 * S:3 * S], sw3[:].indirect(l_offs3[:]))
        for q in range(4):
            nc.scalar.dma_start(
                planes[32 * q:32 * q + 4, :].bitcast(I32).rearrange("r (a n) -> r a n", a=2),
                gsc[8 * q:8 * q + 8, :].bitcast(I32))
        sc2 = [planes[:, 0:S], planes[:, 3 * S:4 * S]]
        sc1 = planes[:, S:2 * S]
        sc3 = planes[:, 2 * S:3 * S]

        wsc = held("wsc", [P, 2 * H], U8)
        nc.vector.tensor_copy(wsc[:].rearrange("p (g t m) -> p g t m", g=4, t=4),
                              wsc_raw[:].rearrange("p (g m t) -> p g t m", g=4, t=4))
        wb_sb = held("wb_sb", [P, 2 * H], U16)
        nc.vector.tensor_copy(wb_sb[:].rearrange("p (g t m) -> p g t m", g=4, t=4),
                              wb_raw[:].rearrange("p (g m t) -> p g t m", g=4, t=4))
        wd_sb = held("wd_sb", [P, H], I32)
        nc.vector.tensor_copy(wd_sb[:].rearrange("p (g t c i) -> p g c t i", g=2, t=4, i=4),
                              wd_raw[:].rearrange("p (g c i t) -> p g c t i", g=2, t=4, i=4))
        turns = held("turns", [P, 2, 4], F32)
        nc.vector.tensor_scalar(turns[:], swing_sb[:], 1.0 / (2.0 * math.pi), None, ALU.mult)

        def round_weight(raw):
            bf = ring("wbf", 2, "wbf", [P, 4 * BANK], BF16)
            nc.scalar.copy(bf[:].rearrange("p (t m j) -> p m j t", t=4, j=4),
                           raw.rearrange("p j (m t) -> p m j t", t=4))
            return bf

        def quantise(bf, codes, scales):
            nc.vector.quantize_mx(out=codes.bitcast(E4M3), scales=scales, in_=bf)

        def gather_words(name, table, idx):
            g = held(name, [P, S], U32)
            nc.vector.tensor_copy(g[:], table[:].bitcast(U32).indirect(idx[:]))
            return g

        def first_stage(i, passes, func, name):
            cols = slice(i * P, (i + 1) * P)
            win = row4k(name, [P, S], F32)
            for half in range(S // BANK):
                js = slice(half * BANK, (half + 1) * BANK)
                acc = psum.tile([P, BANK], F32, name="acc", tag="acc")
                for n, (w, ws, v, vs) in enumerate(passes):
                    nc.tensor.matmul_mx(out=acc[:], lhsT=w(cols), lhsT_scale=ws(cols),
                                        rhs=v[:, js].bitcast(E4M3), rhs_scale=vs[:, js],
                                        start=(n == 0), stop=(n == len(passes) - 1))
                nc.scalar.activation(win[:, js], acc[:], func)
            return win

        wa_q = held("wa_q", [P, H], U32)
        wa_s = held("wa_s", [P, H], U8)
        for h in range(2):
            cs = slice(h * BANK, (h + 1) * BANK)
            quantise(round_weight(wa_raw[:, h])[:], wa_q[:, cs], wa_s[:, cs])
        v1 = gather_words("v1", tw1, l_offs)
        tw3 = big("tw3", [P, T], I32)
        nc.sync.dma_start(tw3[:], words_i32(tab3_words, 0))
        a1_group = [held("a1_%d" % b, [P, 4, J], F32) for b in range(2)]
        a1 = [a1_group[i // 4][:, i % 4, :] for i in range(TILES)]
        v2 = []
        for i in range(TILES):
            win = first_stage(i, [(lambda c: wa_q[:, c].bitcast(E4M3), lambda c: wa_s[:, c], v1, sc1)],
                              ACT.Copy, "win_a")
            nc.vector.tensor_copy(a1[i], win[:].indirect(l_pos1[:]))
            if i in (1, 4):
                a = len(v2)
                v2.append(gather_words("v2_%d" % a, tw2[a], l_offs2))

        wz_raw = []
        for b in range(2):
            t = big("wz_raw%d" % b, [P, 2, 4, BANK], F32)
            for h in range(2):
                load_weight(t, wz[b * 512:(b + 1) * 512, :], h)
            wz_raw.append(t)

        b_passes = [(lambda c, a=a: wb_sb[:, a * H + c.start:a * H + c.stop].bitcast(E2M1),
                     lambda c, a=a: wsc[:, a * H + c.start:a * H + c.stop], v2[a], sc2[a]) for a in range(2)]
        b_win = [first_stage(i, b_passes, ACT.Tanh, "win_b") for i in range(TILES)]
        v3 = gather_words("v3", tw3, l_offs3)
        d_pass = [(lambda c: wd_sb[:, c].bitcast(E4M3), lambda c: wsc[4:P, c], v3, sc3)]
        d_win = []
        sq = [held("sq_%d" % b, [P, 4, J], F32) for b in range(2)]
        wz_q = held("wz_q", [P, 2 * H], U32)
        wz_s = held("wz_s", [P, 2 * H], U8)
        wz_bf = {}

        def round_wz(n):
            wz_bf[n] = round_weight(wz_raw[n // 2][:, n % 2])

        def quantise_wz(n):
            cs = slice(n * BANK, (n + 1) * BANK)
            quantise(wz_bf[n][:], wz_q[:, cs], wz_s[:, cs])

        def cosine(half, b):
            part = sq[b][:, :, half * HALF:(half + 1) * HALF]
            nc.scalar.activation(part, part, ACT.Abs)
            nc.scalar.activation(part, part, ACT.Sin, scale=-2.0 * math.pi, bias=math.pi / 2.0)

        picked = {}
        whole = {}
        for step in range(TILES + 2):
            if step < TILES:
                picked[step] = row2k("picked", [P, J], F32)
                nc.vector.tensor_copy(picked[step][:], b_win[step][:].indirect(l_pos2[:]))
                d_win.append(first_stage(step, d_pass, ACT.Copy, "win_d"))
            if step in (2, 4, 7):
                round_wz(len(wz_bf))
            i = step - 1
            if 0 <= i < TILES:
                whole[i] = row2k("whole", [P, J], I32)
                nc.gpsimd.tensor_scalar(whole[i][:], picked[i][:], turns[:, i // 4, i % 4:i % 4 + 1], 0.0,
                                        ALU.mult, ALU.add)
            i = step - 2
            if 0 <= i < TILES:
                nc.vector.scalar_tensor_tensor(sq[i // 4][:, i % 4, :], picked[i][:],
                                               turns[:, i // 4, i % 4:i % 4 + 1],
                                               whole[i][:], ALU.mult, ALU.subtract)
            if step == 4:
                quantise_wz(0)
            if step == 6:
                quantise_wz(1)

        out_v = out.rearrange("(h m t) j -> h m t j", h=2, t=4)

        def join(half, b, sums):
            js = slice(half * HALF, (half + 1) * HALF)
            idx = l_pos3[:, half * (HALF // 16):(half + 1) * (HALF // 16)]
            z32 = ring("z32", 2, "z32", [P, 4, HALF], F32)
            for t in range(4):
                i = 4 * b + t
                nc.vector.tensor_tensor(sums[:, t, :], d_win[i][:].indirect(idx), a1[i][:, js], ALU.add)
            nc.vector.tensor_tensor(z32[:], sq[b][:, :, js], sums, ALU.mult)
            zbf = row2k("zbf", [P, 4 * HALF], BF16)
            nc.scalar.copy(zbf[:].rearrange("p (c i t) -> p c t i", i=4, t=4),
                           z32[:].rearrange("p t (c i) -> p c t i", i=4))
            codes = held("z_q%d%d" % (half, b), [P, HALF], U32)
            scales = held("z_s%d%d" % (half, b), [P, HALF], U8)
            return zbf, codes, scales

        def fresh_sums():
            return ring("sum", 2, "sum", [P, 4, HALF], F32)[:]

        def product(acc, i, b, zq):
            cs = slice(b * H + i * P, b * H + (i + 1) * P)
            nc.tensor.matmul_mx(out=acc, lhsT=wz_q[:, cs].bitcast(E4M3), lhsT_scale=wz_s[:, cs],
                                rhs=zq[b][1][:].bitcast(E4M3), rhs_scale=zq[b][2][:],
                                start=(b == 0), stop=(b == 1))

        def floor_and_store(half, accs, pairs):
            js = slice(half * HALF, (half + 1) * HALF)
            for pair in pairs:
                res = row2k("res", [P, 2, HALF], F32)
                for u in range(2):
                    i = 2 * pair + u
                    nc.vector.scalar_tensor_tensor(res[:, u, :], a1[i][:, js], keep_sb[:, i // 4, i % 4:i % 4 + 1],
                                                   accs[i], ALU.mult, ALU.max)
                t0 = 2 * (pair % 2)
                nc.sync.dma_start(out_v[pair // 2, :, t0:t0 + 2, js], res[:])

        cosine(0, 0)
        quantise_wz(2)
        round_wz(3)
        cosine(0, 1)
        z0 = [join(0, 0, fresh_sums())]
        quantise_wz(3)
        cosine(1, 0)
        z0.append(join(0, 1, fresh_sums()))
        quantise(z0[0][0][:], z0[0][1][:], z0[0][2][:])
        cosine(1, 1)
        z1 = [join(1, 0, fresh_sums())]
        quantise(z0[1][0][:], z0[1][1][:], z0[1][2][:])
        accs0 = []
        for pair in range(TILES // 2):
            bank = psum.tile([P, BANK], F32, name="acc", tag="acc")
            for u in range(2):
                accs0.append(bank[:, u * HALF:(u + 1) * HALF])
                for b in range(2):
                    product(accs0[-1], 2 * pair + u, b, z0)
        floor_and_store(0, accs0, (0, 1))
        quantise(z1[0][0][:], z1[0][1][:], z1[0][2][:])
        z1.append(join(1, 1, a1_group[0][:, :, 0:HALF]))
        floor_and_store(0, accs0, (2, 3))
        accs1 = []
        for i in range(TILES):
            bank = psum.tile([P, BANK], F32, name="acc", tag="acc")
            accs1.append(bank[:, 0:HALF])
            product(accs1[i], i, 0, z1)
        quantise(z1[1][0][:], z1[1][1][:], z1[1][2][:])
        for i in range(TILES):
            product(accs1[i], i, 1, z1)
        floor_and_store(1, accs1, range(TILES // 2))
